import numpy as np
import ml_dtypes


def mxq(x, axis, fmt="e4m3"):
    dtype, down = {"e4m3": (ml_dtypes.float8_e4m3fn, 7), "e5m2": (ml_dtypes.float8_e5m2, 14)}[fmt]
    v = np.moveaxis(np.asarray(x, np.float32).astype(ml_dtypes.bfloat16).astype(np.float64), axis, -1)
    blocks = v.reshape(v.shape[:-1] + (-1, 32))
    amax = np.abs(blocks).max(-1, keepdims=True)
    byte = np.maximum(np.where(amax > 0, np.frexp(amax)[1] - 1 + 127, 0) - down, 1)
    scale = np.exp2(byte - 127.0)
    codes = (blocks / scale).astype(np.float32).astype(dtype).astype(np.float64)
    return np.moveaxis((codes * scale).reshape(v.shape), -1, axis)


WIDE = False


def mx_kscale(k):
    if not WIDE:
        return np.ones(k)
    levels = np.array([30, -30])
    if k % 512:
        return np.exp2(np.random.permutation(np.resize(levels, k // 32))).repeat(32)
    a = np.empty((k // 512, 16))
    for p in range(k // 512):
        a[p, :8] = np.random.permutation(np.resize(levels, 8))
        for g in range(8):
            far = levels[np.abs(levels - a[p, g]) >= 10]
            a[p, g + 8] = far[np.random.randint(len(far))]
    return np.exp2(a.ravel()).repeat(32)


def f64(x):
    return np.asarray(x).astype(np.float64)


def striped(idx):
    return np.tile(np.asarray(idx).reshape(-1, 16).T, (8, 1)).astype(np.uint16)


def unstriped(offs):
    return offs[:16].T.reshape(-1).astype(np.int64)


def striped8(idx):
    return np.asarray(idx).reshape(8, -1, 16).transpose(0, 2, 1).reshape(128, -1).astype(np.uint16)


def unstriped8(offs):
    return offs.reshape(8, 16, -1).transpose(0, 2, 1).reshape(8, -1).astype(np.int64)


def pick8(x, idx, run):
    r = np.arange(len(x))
    return x[r[:, None], idx[r % (8 * run) // run]]


E2M1 = np.array([0.0, 0.5, 1.0, 1.5, 2.0, 3.0, 4.0, 6.0, -0.0, -0.5, -1.0, -1.5, -2.0, -3.0, -4.0, -6.0])


def pack_weight(w, fmt):
    k, n = w.shape
    w = f64(np.asarray(w, np.float32).astype(ml_dtypes.bfloat16)).reshape(k // 32, 32, n)
    amax = np.abs(w).max(1)
    if fmt in ("e4m3", "e5m2"):
        byte = np.frexp(amax)[1] - 1 + 127 - (7 if fmt == "e4m3" else 14)
    else:
        mant, ex = np.frexp(amax / 6.0)
        byte = np.where(mant > 0.5, ex, ex - 1) + 127
    byte = np.clip(np.where(amax > 0, byte, 1), 1, 254)
    scaled = (w * np.exp2(127.0 - byte)[:, None, :]).reshape(k, n).astype(np.float32)
    by_word = np.ascontiguousarray(scaled.reshape(k // 512, 128, 4, n).transpose(0, 1, 3, 2))
    if fmt in ("e4m3", "e5m2"):
        words = by_word.astype(ml_dtypes.float8_e4m3fn if fmt == "e4m3" else ml_dtypes.float8_e5m2).view(np.uint8)
    else:
        c = by_word.astype(ml_dtypes.float4_e2m1fn).view(np.uint8) & 0xF
        words = (c[..., 0::2] | (c[..., 1::2] << 4)).reshape(k // 512, 128, 2 * n)
    return np.ascontiguousarray(words), np.ascontiguousarray(byte.astype(np.uint8).reshape(k // 512, 16, n))


def unpack_weight(words, scales, fmt):
    g, _, n = scales.shape
    words = np.ascontiguousarray(words).reshape(g, 128, n, -1)
    if fmt in ("e4m3", "e5m2"):
        vals = words.view(ml_dtypes.float8_e4m3fn if fmt == "e4m3" else ml_dtypes.float8_e5m2).astype(np.float64)
    else:
        nib = np.empty((g, 128, n, 4), np.uint8)
        nib[..., 0::2] = words & 0xF
        nib[..., 1::2] = words >> 4
        vals = E2M1[nib]
    vals = vals * np.repeat(np.exp2(scales.astype(np.float64) - 127.0), 8, axis=1)[..., None]
    return vals.transpose(0, 1, 3, 2).reshape(g * 512, n)


K, T, J, R, V, O, N, S, E = 512, 1024, 256, 512, 1024, 128, 256, 1024, 1024


def setup_inputs():
    n = np.random.standard_normal
    idx = np.random.permutation(V)[:R]
    idx2 = np.random.permutation(T)[:J]
    idx3 = np.stack([np.random.permutation(J)[:O] for _ in range(8)])
    idx4 = np.stack([np.random.permutation(J)[:O] for _ in range(8)])
    idx5 = np.random.permutation(S)[:N]
    idx6 = np.random.permutation(E)[:O]
    fk = mx_kscale(K)
    fr = mx_kscale(R)
    tr = np.ones(V)
    tr[idx] = fr
    xtp = pack_weight(n((K, T)) / fk[:, None], "e5m2")
    wtp = pack_weight(n((K, V)) * 1 / np.sqrt(K) * fk[:, None] * tr, "e2m1")
    w2p = pack_weight(n((K, R)) * 1 / np.sqrt(K) * fk[:, None], "e4m3")
    vsp = pack_weight(n((R, S)) * 1 / np.sqrt(R) / fr[:, None], "e2m1")
    return {
        "xt_words": xtp[0],
        "xt_scales": xtp[1],
        "wt_words": wtp[0],
        "wt_scales": wtp[1],
        "w2_words": w2p[0],
        "w2_scales": w2p[1],
        "vs_words": vsp[0],
        "vs_scales": vsp[1],
        "offs": striped(idx),
        "offs2": striped(idx2),
        "offs3": striped8(idx3),
        "offs4": striped8(idx4),
        "offs5": striped(idx5),
        "offs6": striped(idx6),
    }


def reference(xt_words, xt_scales, wt_words, wt_scales, w2_words, w2_scales, vs_words, vs_scales, offs, offs2, offs3, offs4, offs5, offs6):
    idx = unstriped(offs)
    idx2 = unstriped(offs2)
    idx3 = unstriped8(offs3)
    idx4 = unstriped8(offs4)
    idx5 = unstriped(offs5)
    idx6 = unstriped(offs6)
    xtu = unpack_weight(xt_words, xt_scales, "e5m2")
    wtu = unpack_weight(wt_words, wt_scales, "e2m1")
    w2u = unpack_weight(w2_words, w2_scales, "e4m3")
    vsu = unpack_weight(vs_words, vs_scales, "e2m1")
    wtidxg = wtu[:, idx]
    xtidx2g = xtu[:, idx2]
    a = wtidxg.T @ xtidx2g
    b = w2u.T @ xtidx2g
    lb = b[:, 0:1]
    la = a[:, 0:1]
    hid = np.abs(pick8(a, idx3, 64) * lb - pick8(b, idx4, 64) * la)
    vsidx5g = vsu[:, idx5]
    hidq = mxq(hid, 0, "e4m3")
    p = vsidx5g.T @ hidq
    y = np.zeros((N, E))
    y[:, idx6] = p
    return y

@@ -1,0 +1,177 @@
+from contextlib import ExitStack
+
+import concourse.mybir as mybir
+
+K, T, J, R, V, O, N, S, E = 512, 1024, 256, 512, 1024, 128, 256, 1024, 1024
+FLOPS = 2 * K * R * J * 2 + 2 * R * N * O
+
+F32 = mybir.dt.float32
+BF16 = mybir.dt.bfloat16
+I32 = mybir.dt.int32
+U32 = mybir.dt.uint32
+U16 = mybir.dt.uint16
+U8 = mybir.dt.uint8
+E4M3 = mybir.dt.float8_e4m3fn_x4
+E5M2 = mybir.dt.float8_e5m2_x4
+E2M1 = mybir.dt.float4_e2m1fn_x4
+ALU = mybir.AluOpType
+ACT = mybir.ActivationFunctionType
+
+P = 128
+PACK = 4
+
+
+def tile_list_groupleads_storeleads_store_scattered_kernel(
+    tc, xt_words, xt_scales, wt_words, wt_scales, w2_words, w2_scales, vs_words, vs_scales,
+    offs, offs2, offs3, offs4, offs5, offs6, out,
+):
+    nc = tc.nc
+    with ExitStack() as ctx:
+        sb = ctx.enter_context(tc.tile_pool(name="sb", bufs=1))
+        ps = ctx.enter_context(tc.psum_pool(name="ps", bufs=1))
+
+        def tile(name, cols, dtype, tag=None):
+            return sb.tile([P, cols], dtype, name=name, tag=tag or name, align_bytes=64)
+
+        def load_list(name, src):
+            lst = sb.tile(list(src.shape), U16, name=name)
+            nc.sync.dma_start(lst[:], src)
+            return lst
+
+        def zeroed_plane(name, cols, engine):
+            plane = tile(name, cols, U8)
+            engine.memset(plane[:].bitcast(I32), 0)
+            return plane
+
+        def load_scales(plane, scales, queues):
+            for q in range(4):
+                queues[q].dma_start(
+                    out=plane[32 * q : 32 * q + 4, :].bitcast(I32),
+                    in_=scales[0, 4 * q : 4 * q + 4, :].bitcast(I32),
+                )
+
+        def deal(engine_copy, dst, src, run):
+            engine_copy(
+                out=dst[:].rearrange("p (t c i) -> p c t i", t=PACK, i=run),
+                in_=src[:].rearrange("p (c i t) -> p c t i", t=PACK, i=run),
+            )
+
+        wt_plane = zeroed_plane("wt_plane", V, nc.vector)
+        w2_plane = zeroed_plane("w2_plane", R, nc.gpsimd)
+        xt_plane = zeroed_plane("xt_plane", T, nc.vector)
+        pages = [tile("page%d" % h, E, F32) for h in range(N // P)]
+        nc.vector.memset(pages[0][:].bitcast(I32), 0)
+        nc.vector.memset(pages[1][:].bitcast(I32), 0)
+
+        xt_tab = tile("xt_tab", T, U32)
+        w2_tab = tile("w2_tab", R, U32)
+        wt_tab = tile("wt_tab", V, U16)
+        vs_tab = tile("vs_tab", S, U16)
+
+        on_sync = [nc.sync] * 4
+        idx = load_list("idx", offs)
+        load_scales(wt_plane, wt_scales, on_sync)
+        idx2 = load_list("idx2", offs2)
+        nc.sync.dma_start(out=xt_tab[:].bitcast(I32), in_=xt_words[0].rearrange("p n t -> p (n t)").bitcast(I32))
+        nc.sync.dma_start(out=w2_tab[:].bitcast(I32), in_=w2_words[0].rearrange("p n t -> p (n t)").bitcast(I32))
+        load_scales(xt_plane, xt_scales, on_sync)
+        load_scales(w2_plane, w2_scales, [nc.sync, nc.sync, nc.gpsimd, nc.gpsimd])
+        vs_plane = zeroed_plane("vs_plane", S, nc.gpsimd)
+        nc.sync.dma_start(out=wt_tab[:].bitcast(I32), in_=wt_words[0].bitcast(I32))
+        idx3 = load_list("idx3", offs3)
+        idx4 = load_list("idx4", offs4)
+        idx5 = load_list("idx5", offs5)
+        nc.sync.dma_start(out=vs_tab[:].bitcast(I32), in_=vs_words[0].bitcast(I32))
+        load_scales(vs_plane, vs_scales, on_sync)
+        idx6 = load_list("idx6", offs6)
+
+        wt_sc = tile("wt_sc", R, U8)
+        nc.vector.tensor_copy(wt_sc[:].rearrange("p (t m) -> p m t", t=PACK), wt_plane[:].indirect(idx[:]))
+        xt_w = tile("xt_w", J, U32)
+        nc.vector.tensor_copy(xt_w[:], xt_tab[:].indirect(idx2[:]))
+        xt_sc = tile("xt_sc", J, U8)
+        nc.vector.tensor_copy(xt_sc[:], xt_plane[:].indirect(idx2[:]))
+        w2_w = tile("w2_w", R, U32)
+        deal(nc.scalar.copy, w2_w, w2_tab, 4)
+        w2_sc = tile("w2_sc", R, U8)
+        deal(nc.vector.tensor_copy, w2_sc, w2_plane, 16)
+
+        b_ps = [ps.tile([P, 2, J], F32, name="b_ps%d" % u) for u in range(2)]
+        b_sb = [tile("b%d" % t, J, F32) for t in range(PACK)]
+        for t in range(PACK):
+            cols = slice(t * P, (t + 1) * P)
+            nc.tensor.matmul_mx(
+                out=b_ps[t // 2][:, t % 2, :],
+                lhsT=w2_w[:, cols].bitcast(E4M3), lhsT_scale=w2_sc[:, cols],
+                rhs=xt_w[:].bitcast(E5M2), rhs_scale=xt_sc[:],
+                start=True, stop=True,
+            )
+        for t in range(PACK):
+            nc.scalar.activation(out=b_sb[t][:], in_=b_ps[t // 2][:, t % 2, :], func=ACT.Copy)
+
+        wt_listed = tile("wt_listed", R, U16)
+        nc.vector.tensor_copy(wt_listed[:], wt_tab[:].indirect(idx[:]))
+        wt_w = tile("wt_w", R, U16)
+        deal(nc.vector.tensor_copy, wt_w, wt_listed, 8)
+
+        a_ps = [ps.tile([P, J], F32, name="a_ps%d" % t) for t in range(PACK)]
+        a_sb = [tile("a%d" % t, J, F32) for t in range(PACK)]
+        for t in range(PACK):
+            cols = slice(t * P, (t + 1) * P)
+            nc.tensor.matmul_mx(
+                out=a_ps[t][:],
+                lhsT=wt_w[:, cols].bitcast(E2M1), lhsT_scale=wt_sc[:, cols],
+                rhs=xt_w[:].bitcast(E5M2), rhs_scale=xt_sc[:],
+                start=True, stop=True,
+            )
+            nc.vector.tensor_copy(a_sb[t][:], a_ps[t][:])
+
+        vs_w = tile("vs_w", N, U16, "wt_w")
+        nc.vector.tensor_copy(vs_w[:], vs_tab[:].indirect(idx5[:]))
+        vs_sc = tile("vs_sc", N, U8, "wt_sc")
+        nc.vector.tensor_copy(vs_sc[:], vs_plane[:].indirect(idx5[:]))
+
+        diff = tile("diff", PACK * O, F32)
+        for t in range(PACK):
+            first = tile("first%d" % t, O, F32, "vs_tab" if t == PACK - 1 else None)
+            second = tile("second%d" % t, O, F32, "vs_plane" if t == PACK - 1 else None)
+            nc.scalar.activation(out=first[:], in_=a_sb[t][:].indirect(idx3[:]), func=ACT.Copy, scale=b_sb[t][:, 0:1])
+            nc.scalar.activation(out=second[:], in_=b_sb[t][:].indirect(idx4[:]), func=ACT.Copy, scale=a_sb[t][:, 0:1])
+            nc.vector.tensor_tensor(out=diff[:, t * O : (t + 1) * O], in0=first[:], in1=second[:], op=ALU.subtract)
+
+        hid = tile("hid", O * PACK, BF16)
+        half = O // 2
+        woven = hid[:].rearrange("p (o t) -> p o t", t=PACK)
+        planes = diff[:].rearrange("p (t o) -> p o t", t=PACK)
+        nc.scalar.activation(
+            out=hid[:, 0 : half * PACK].rearrange("p (c i t) -> p c t i", t=PACK, i=4),
+            in_=planes[:, 0:half, :].rearrange("p (c i) t -> p c t i", i=4),
+            func=ACT.Abs,
+        )
+        nc.vector.scalar_tensor_tensor(
+            out=woven[:, half:O, :], in0=planes[:, half:O, :], scalar=-1.0, in1=planes[:, half:O, :],
+            op0=ALU.mult, op1=ALU.max,
+        )
+        hid_w = tile("hid_w", O, U32)
+        hid_sc = tile("hid_sc", O, U8)
+        nc.vector.quantize_mx(out=hid_w[:].bitcast(E4M3), scales=hid_sc[:], in_=hid[:])
+
+        placed = []
+        for h in range(N // P):
+            cols = slice(h * P, (h + 1) * P)
+            p_ps = ps.tile([P, O], F32, name="p_ps%d" % h)
+            nc.tensor.matmul_mx(
+                out=p_ps[:],
+                lhsT=vs_w[:, cols].bitcast(E2M1), lhsT_scale=vs_sc[:, cols],
+                rhs=hid_w[:].bitcast(E4M3), rhs_scale=hid_sc[:],
+                start=True, stop=True,
+            )
+            placed.append(p_ps)
+        p0 = tile("p0", O, F32)
+        nc.vector.tensor_copy(p0[:], placed[0][:])
+        nc.vector.tensor_copy(pages[0][:].indirect(idx6[:]), p0[:])
+        nc.sync.dma_start(out=out[0:P, :], in_=pages[0][:])
+        p1 = tile("p1", O, F32)
+        nc.scalar.activation(out=p1[:], in_=placed[1][:], func=ACT.Copy)
+        nc.scalar.activation(out=pages[1][:].indirect(idx6[:]), in_=p1[:], func=ACT.Copy)
+        nc.scalar.dma_start(out=out[P : 2 * P, :], in_=pages[1][:])

@@ -72,72 +72,74 @@ def tile_list_groupleads_storeleads_store_scattered_kernel(
         idx = load_list("idx", offs)
         load_scales(wt_plane, wt_scales, on_sync)
         idx2 = load_list("idx2", offs2)
-        nc.sync.dma_start(out=xt_tab[:].bitcast(I32), in_=xt_words[0].rearrange("p n t -> p (n t)").bitcast(I32))
-        nc.sync.dma_start(out=w2_tab[:].bitcast(I32), in_=w2_words[0].rearrange("p n t -> p (n t)").bitcast(I32))
-        load_scales(xt_plane, xt_scales, on_sync)
-        load_scales(w2_plane, w2_scales, [nc.sync, nc.sync, nc.gpsimd, nc.gpsimd])
-        vs_plane = zeroed_plane("vs_plane", S, nc.gpsimd)
         nc.sync.dma_start(out=wt_tab[:].bitcast(I32), in_=wt_words[0].bitcast(I32))
-        idx3 = load_list("idx3", offs3)
-        idx4 = load_list("idx4", offs4)
+        nc.sync.dma_start(out=xt_tab[:].bitcast(I32), in_=xt_words[0].rearrange("p n t -> p (n t)").bitcast(I32))
+        load_scales(xt_plane, xt_scales, on_sync)
+        nc.sync.dma_start(out=w2_tab[:].bitcast(I32), in_=w2_words[0].rearrange("p n t -> p (n t)").bitcast(I32))
         idx5 = load_list("idx5", offs5)
         nc.sync.dma_start(out=vs_tab[:].bitcast(I32), in_=vs_words[0].bitcast(I32))
+        load_scales(w2_plane, w2_scales, on_sync)
+        vs_plane = zeroed_plane("vs_plane", S, nc.gpsimd)
+        idx3 = load_list("idx3", offs3)
+        idx4 = load_list("idx4", offs4)
         load_scales(vs_plane, vs_scales, on_sync)
         idx6 = load_list("idx6", offs6)
 
         wt_sc = tile("wt_sc", R, U8)
         nc.vector.tensor_copy(wt_sc[:].rearrange("p (t m) -> p m t", t=PACK), wt_plane[:].indirect(idx[:]))
+        wt_listed = tile("wt_listed", R, U16)
+        nc.vector.tensor_copy(wt_listed[:], wt_tab[:].indirect(idx[:]))
         xt_w = tile("xt_w", J, U32)
         nc.vector.tensor_copy(xt_w[:], xt_tab[:].indirect(idx2[:]))
+        wt_w = tile("wt_w", R, U16)
+        deal(nc.vector.tensor_copy, wt_w, wt_listed, 8)
         xt_sc = tile("xt_sc", J, U8)
         nc.vector.tensor_copy(xt_sc[:], xt_plane[:].indirect(idx2[:]))
         w2_w = tile("w2_w", R, U32)
         deal(nc.scalar.copy, w2_w, w2_tab, 4)
         w2_sc = tile("w2_sc", R, U8)
         deal(nc.vector.tensor_copy, w2_sc, w2_plane, 16)
+        vs_w = tile("vs_w", N, U16, "w2_plane")
+        nc.vector.tensor_copy(vs_w[:], vs_tab[:].indirect(idx5[:]))
 
-        b_ps = [ps.tile([P, 2, J], F32, name="b_ps%d" % u) for u in range(2)]
+        def product(acc, words, fmt, scales, t):
+            cols = slice(t * P, (t + 1) * P)
+            nc.tensor.matmul_mx(
+                out=acc,
+                lhsT=words[:, cols].bitcast(fmt), lhsT_scale=scales[:, cols],
+                rhs=xt_w[:].bitcast(E5M2), rhs_scale=xt_sc[:],
+                start=True, stop=True,
+            )
+
+        banks = [ps.tile([P, 2, J], F32, name="bank%d" % u) for u in range(6)]
+        a_ps = [banks[0][:, 0, :], banks[1][:, 0, :], banks[3][:, 1, :], banks[4][:, 1, :]]
+        b_ps = [banks[2][:, 0, :], banks[3][:, 0, :], banks[4][:, 0, :], banks[5][:, 0, :]]
+        for which, t in (("a", 0), ("a", 1), ("b", 0), ("b", 1), ("a", 2), ("b", 2), ("a", 3), ("b", 3)):
+            if which == "a":
+                product(a_ps[t], wt_w, E2M1, wt_sc, t)
+            else:
+                product(b_ps[t], w2_w, E4M3, w2_sc, t)
+        a_sb = [tile("a%d" % t, J, F32) for t in range(PACK)]
         b_sb = [tile("b%d" % t, J, F32) for t in range(PACK)]
         for t in range(PACK):
-            cols = slice(t * P, (t + 1) * P)
-            nc.tensor.matmul_mx(
-                out=b_ps[t // 2][:, t % 2, :],
-                lhsT=w2_w[:, cols].bitcast(E4M3), lhsT_scale=w2_sc[:, cols],
-                rhs=xt_w[:].bitcast(E5M2), rhs_scale=xt_sc[:],
-                start=True, stop=True,
-            )
-        for t in range(PACK):
-            nc.scalar.activation(out=b_sb[t][:], in_=b_ps[t // 2][:, t % 2, :], func=ACT.Copy)
+            if t < 2:
+                nc.scalar.activation(out=a_sb[t][:], in_=a_ps[t], func=ACT.Copy)
+            else:
+                nc.vector.tensor_copy(a_sb[t][:], a_ps[t])
+            nc.vector.tensor_copy(b_sb[t][:], b_ps[t])
 
-        wt_listed = tile("wt_listed", R, U16)
-        nc.vector.tensor_copy(wt_listed[:], wt_tab[:].indirect(idx[:]))
-        wt_w = tile("wt_w", R, U16)
-        deal(nc.vector.tensor_copy, wt_w, wt_listed, 8)
-
-        a_ps = [ps.tile([P, J], F32, name="a_ps%d" % t) for t in range(PACK)]
-        a_sb = [tile("a%d" % t, J, F32) for t in range(PACK)]
-        for t in range(PACK):
-            cols = slice(t * P, (t + 1) * P)
-            nc.tensor.matmul_mx(
-                out=a_ps[t][:],
-                lhsT=wt_w[:, cols].bitcast(E2M1), lhsT_scale=wt_sc[:, cols],
-                rhs=xt_w[:].bitcast(E5M2), rhs_scale=xt_sc[:],
-                start=True, stop=True,
-            )
-            nc.vector.tensor_copy(a_sb[t][:], a_ps[t][:])
-
-        vs_w = tile("vs_w", N, U16, "wt_w")
-        nc.vector.tensor_copy(vs_w[:], vs_tab[:].indirect(idx5[:]))
-        vs_sc = tile("vs_sc", N, U8, "wt_sc")
+        vs_sc = tile("vs_sc", N, U8, "w2_sc")
         nc.vector.tensor_copy(vs_sc[:], vs_plane[:].indirect(idx5[:]))
 
-        diff = tile("diff", PACK * O, F32)
+        first = tile("first", PACK * O, F32)
+        second = tile("second", PACK * O, F32)
+        diff = tile("diff", PACK * O, F32, "vs_plane")
         for t in range(PACK):
-            first = tile("first%d" % t, O, F32, "vs_tab" if t == PACK - 1 else None)
-            second = tile("second%d" % t, O, F32, "vs_plane" if t == PACK - 1 else None)
-            nc.scalar.activation(out=first[:], in_=a_sb[t][:].indirect(idx3[:]), func=ACT.Copy, scale=b_sb[t][:, 0:1])
-            nc.scalar.activation(out=second[:], in_=b_sb[t][:].indirect(idx4[:]), func=ACT.Copy, scale=a_sb[t][:, 0:1])
-            nc.vector.tensor_tensor(out=diff[:, t * O : (t + 1) * O], in0=first[:], in1=second[:], op=ALU.subtract)
+            cols = slice(t * O, (t + 1) * O)
+            nc.scalar.activation(out=first[:, cols], in_=a_sb[t][:].indirect(idx3[:]), func=ACT.Copy, scale=b_sb[t][:, 0:1])
+            nc.scalar.activation(out=second[:, cols], in_=b_sb[t][:].indirect(idx4[:]), func=ACT.Copy, scale=a_sb[t][:, 0:1])
+        for cols in (slice(0, 3 * O), slice(3 * O, 4 * O)):
+            nc.vector.tensor_tensor(out=diff[:, cols], in0=first[:, cols], in1=second[:, cols], op=ALU.subtract)
 
         hid = tile("hid", O * PACK, BF16)
         half = O // 2

@@ -60,8 +60,8 @@ def tile_list_groupleads_storeleads_store_scattered_kernel(
         w2_plane = zeroed_plane("w2_plane", R, nc.gpsimd)
         xt_plane = zeroed_plane("xt_plane", T, nc.vector)
         pages = [tile("page%d" % h, E, F32) for h in range(N // P)]
-        nc.vector.memset(pages[0][:].bitcast(I32), 0)
-        nc.vector.memset(pages[1][:].bitcast(I32), 0)
+        for page in pages:
+            nc.vector.memset(page[:].bitcast(I32), 0)
 
         xt_tab = tile("xt_tab", T, U32)
         w2_tab = tile("w2_tab", R, U32)
@@ -69,10 +69,10 @@ def tile_list_groupleads_storeleads_store_scattered_kernel(
         vs_tab = tile("vs_tab", S, U16)
 
         on_sync = [nc.sync] * 4
+        nc.sync.dma_start(out=wt_tab[:].bitcast(I32), in_=wt_words[0].bitcast(I32))
         idx = load_list("idx", offs)
         load_scales(wt_plane, wt_scales, on_sync)
         idx2 = load_list("idx2", offs2)
-        nc.sync.dma_start(out=wt_tab[:].bitcast(I32), in_=wt_words[0].bitcast(I32))
         nc.sync.dma_start(out=xt_tab[:].bitcast(I32), in_=xt_words[0].rearrange("p n t -> p (n t)").bitcast(I32))
         load_scales(xt_plane, xt_scales, on_sync)
         nc.sync.dma_start(out=w2_tab[:].bitcast(I32), in_=w2_words[0].rearrange("p n t -> p (n t)").bitcast(I32))
@@ -85,10 +85,10 @@ def tile_list_groupleads_storeleads_store_scattered_kernel(
         load_scales(vs_plane, vs_scales, on_sync)
         idx6 = load_list("idx6", offs6)
 
-        wt_sc = tile("wt_sc", R, U8)
-        nc.vector.tensor_copy(wt_sc[:].rearrange("p (t m) -> p m t", t=PACK), wt_plane[:].indirect(idx[:]))
         wt_listed = tile("wt_listed", R, U16)
         nc.vector.tensor_copy(wt_listed[:], wt_tab[:].indirect(idx[:]))
+        wt_sc = tile("wt_sc", R, U8)
+        nc.vector.tensor_copy(wt_sc[:].rearrange("p (t m) -> p m t", t=PACK), wt_plane[:].indirect(idx[:]))
         xt_w = tile("xt_w", J, U32)
         nc.vector.tensor_copy(xt_w[:], xt_tab[:].indirect(idx2[:]))
         wt_w = tile("wt_w", R, U16)
@@ -121,6 +121,9 @@ def tile_list_groupleads_storeleads_store_scattered_kernel(
                 product(b_ps[t], w2_w, E4M3, w2_sc, t)
         a_sb = [tile("a%d" % t, J, F32) for t in range(PACK)]
         b_sb = [tile("b%d" % t, J, F32) for t in range(PACK)]
+        lead0 = tile("lead0", 1, F32)
+        nc.vector.tensor_copy(lead0[:], b_ps[0][:, 0:1])
+        leads = [lead0[:]] + [b_sb[t][:, 0:1] for t in range(1, PACK)]
         for t in range(PACK):
             if t < 2:
                 nc.scalar.activation(out=a_sb[t][:], in_=a_ps[t], func=ACT.Copy)
@@ -136,7 +139,7 @@ def tile_list_groupleads_storeleads_store_scattered_kernel(
         diff = tile("diff", PACK * O, F32, "vs_plane")
         for t in range(PACK):
             cols = slice(t * O, (t + 1) * O)
-            nc.scalar.activation(out=first[:, cols], in_=a_sb[t][:].indirect(idx3[:]), func=ACT.Copy, scale=b_sb[t][:, 0:1])
+            nc.scalar.activation(out=first[:, cols], in_=a_sb[t][:].indirect(idx3[:]), func=ACT.Copy, scale=leads[t])
             nc.scalar.activation(out=second[:, cols], in_=b_sb[t][:].indirect(idx4[:]), func=ACT.Copy, scale=a_sb[t][:, 0:1])
         for cols in (slice(0, 3 * O), slice(3 * O, 4 * O)):
             nc.vector.tensor_tensor(out=diff[:, cols], in0=first[:, cols], in1=second[:, cols], op=ALU.subtract)

@@ -3,7 +3,7 @@ from contextlib import ExitStack
 import concourse.mybir as mybir
 
 K, T, J, R, V, O, N, S, E = 512, 1024, 256, 512, 1024, 128, 256, 1024, 1024
-FLOPS = 2 * K * R * J * 2 + 2 * R * N * O
+FLOPS = 2 * (2 * K * R * J) + 2 * R * N * O
 
 F32 = mybir.dt.float32
 BF16 = mybir.dt.bfloat16
@@ -19,6 +19,10 @@ ACT = mybir.ActivationFunctionType
 
 P = 128
 PACK = 4
+QUADRANT = 32
+LINE = 16
+EARLY_TILES = 2
+SCALAR_PLACES = 80
 
 
 def tile_list_groupleads_storeleads_store_scattered_kernel(
@@ -30,36 +34,43 @@ def tile_list_groupleads_storeleads_store_scattered_kernel(
         sb = ctx.enter_context(tc.tile_pool(name="sb", bufs=1))
         ps = ctx.enter_context(tc.psum_pool(name="ps", bufs=1))
 
-        def tile(name, cols, dtype, tag=None):
-            return sb.tile([P, cols], dtype, name=name, tag=tag or name, align_bytes=64)
+        def tile(name, cols, dtype, reuses=None):
+            return sb.tile([P, cols], dtype, name=name, tag=reuses or name, align_bytes=64)
+
+        def part(whole, t):
+            return whole[:, t * P : (t + 1) * P]
 
         def load_list(name, src):
-            lst = sb.tile(list(src.shape), U16, name=name)
-            nc.sync.dma_start(lst[:], src)
-            return lst
+            listed = sb.tile(list(src.shape), U16, name=name)
+            nc.sync.dma_start(listed[:], src)
+            return listed
+
+        def load_words(table, words):
+            nc.sync.dma_start(out=table[:].bitcast(I32), in_=words.bitcast(I32))
 
         def zeroed_plane(name, cols, engine):
             plane = tile(name, cols, U8)
             engine.memset(plane[:].bitcast(I32), 0)
             return plane
 
-        def load_scales(plane, scales, queues):
-            for q in range(4):
-                queues[q].dma_start(
-                    out=plane[32 * q : 32 * q + 4, :].bitcast(I32),
+        def load_scales(plane, scales):
+            for q in range(P // QUADRANT):
+                nc.sync.dma_start(
+                    out=plane[QUADRANT * q : QUADRANT * q + 4, :].bitcast(I32),
                     in_=scales[0, 4 * q : 4 * q + 4, :].bitcast(I32),
                 )
 
-        def deal(engine_copy, dst, src, run):
-            engine_copy(
-                out=dst[:].rearrange("p (t c i) -> p c t i", t=PACK, i=run),
-                in_=src[:].rearrange("p (c i t) -> p c t i", t=PACK, i=run),
+        def deal(copy, dst, src, element_bytes, t0, t1):
+            run = LINE // element_bytes
+            copy(
+                out=dst[:].rearrange("p (t c i) -> p c t i", t=t1 - t0, i=run),
+                in_=src[:].rearrange("p (c i t) -> p c t i", t=PACK, i=run)[:, :, t0:t1, :],
             )
 
         wt_plane = zeroed_plane("wt_plane", V, nc.vector)
         w2_plane = zeroed_plane("w2_plane", R, nc.gpsimd)
         xt_plane = zeroed_plane("xt_plane", T, nc.vector)
-        pages = [tile("page%d" % h, E, F32) for h in range(N // P)]
+        pages = [tile("page%d" % half, E, F32) for half in range(N // P)]
         for page in pages:
             nc.vector.memset(page[:].bitcast(I32), 0)
 
@@ -68,21 +79,20 @@ def tile_list_groupleads_storeleads_store_scattered_kernel(
         wt_tab = tile("wt_tab", V, U16)
         vs_tab = tile("vs_tab", S, U16)
 
-        on_sync = [nc.sync] * 4
-        nc.sync.dma_start(out=wt_tab[:].bitcast(I32), in_=wt_words[0].bitcast(I32))
+        load_words(wt_tab, wt_words[0])
         idx = load_list("idx", offs)
-        load_scales(wt_plane, wt_scales, on_sync)
+        load_scales(wt_plane, wt_scales)
         idx2 = load_list("idx2", offs2)
-        nc.sync.dma_start(out=xt_tab[:].bitcast(I32), in_=xt_words[0].rearrange("p n t -> p (n t)").bitcast(I32))
-        load_scales(xt_plane, xt_scales, on_sync)
-        nc.sync.dma_start(out=w2_tab[:].bitcast(I32), in_=w2_words[0].rearrange("p n t -> p (n t)").bitcast(I32))
+        load_words(xt_tab, xt_words[0].rearrange("p n t -> p (n t)"))
+        load_scales(xt_plane, xt_scales)
+        load_words(w2_tab, w2_words[0].rearrange("p n t -> p (n t)"))
         idx5 = load_list("idx5", offs5)
-        nc.sync.dma_start(out=vs_tab[:].bitcast(I32), in_=vs_words[0].bitcast(I32))
-        load_scales(w2_plane, w2_scales, on_sync)
+        load_words(vs_tab, vs_words[0])
+        load_scales(w2_plane, w2_scales)
         vs_plane = zeroed_plane("vs_plane", S, nc.gpsimd)
         idx3 = load_list("idx3", offs3)
         idx4 = load_list("idx4", offs4)
-        load_scales(vs_plane, vs_scales, on_sync)
+        load_scales(vs_plane, vs_scales)
         idx6 = load_list("idx6", offs6)
 
         wt_listed = tile("wt_listed", R, U16)
@@ -92,91 +102,104 @@ def tile_list_groupleads_storeleads_store_scattered_kernel(
         xt_w = tile("xt_w", J, U32)
         nc.vector.tensor_copy(xt_w[:], xt_tab[:].indirect(idx2[:]))
         wt_w = tile("wt_w", R, U16)
-        deal(nc.vector.tensor_copy, wt_w, wt_listed, 8)
+        deal(nc.vector.tensor_copy, wt_w, wt_listed, 2, 0, PACK)
         xt_sc = tile("xt_sc", J, U8)
         nc.vector.tensor_copy(xt_sc[:], xt_plane[:].indirect(idx2[:]))
         w2_w = tile("w2_w", R, U32)
-        deal(nc.scalar.copy, w2_w, w2_tab, 4)
-        w2_sc = tile("w2_sc", R, U8)
-        deal(nc.vector.tensor_copy, w2_sc, w2_plane, 16)
-        vs_w = tile("vs_w", N, U16, "w2_plane")
+        deal(nc.scalar.copy, w2_w, w2_tab, 4, 0, PACK)
+        w2_sc0 = tile("w2_sc0", P, U8)
+        deal(nc.vector.tensor_copy, w2_sc0, w2_plane, 1, 0, 1)
+        w2_sc_rest = tile("w2_sc_rest", R - P, U8)
+        deal(nc.vector.tensor_copy, w2_sc_rest, w2_plane, 1, 1, PACK)
+        w2_sc = [w2_sc0[:]] + [part(w2_sc_rest, t - 1) for t in range(1, PACK)]
+        vs_w = tile("vs_w", N, U16, reuses="w2_plane")
         nc.vector.tensor_copy(vs_w[:], vs_tab[:].indirect(idx5[:]))
 
-        def product(acc, words, fmt, scales, t):
-            cols = slice(t * P, (t + 1) * P)
+        def first_product(acc, codes, scales):
             nc.tensor.matmul_mx(
                 out=acc,
-                lhsT=words[:, cols].bitcast(fmt), lhsT_scale=scales[:, cols],
+                lhsT=codes, lhsT_scale=scales,
                 rhs=xt_w[:].bitcast(E5M2), rhs_scale=xt_sc[:],
                 start=True, stop=True,
             )
 
-        banks = [ps.tile([P, 2, J], F32, name="bank%d" % u) for u in range(6)]
-        a_ps = [banks[0][:, 0, :], banks[1][:, 0, :], banks[3][:, 1, :], banks[4][:, 1, :]]
-        b_ps = [banks[2][:, 0, :], banks[3][:, 0, :], banks[4][:, 0, :], banks[5][:, 0, :]]
-        for which, t in (("a", 0), ("a", 1), ("b", 0), ("b", 1), ("a", 2), ("b", 2), ("a", 3), ("b", 3)):
-            if which == "a":
-                product(a_ps[t], wt_w, E2M1, wt_sc, t)
-            else:
-                product(b_ps[t], w2_w, E4M3, w2_sc, t)
+        banks = [ps.tile([P, 2, J], F32, name="bank%d" % u) for u in range(EARLY_TILES + PACK)]
+        b_banks = banks[EARLY_TILES:]
+        b_ps = [bank[:, 0, :] for bank in b_banks]
+        a_ps = [banks[t][:, 0, :] if t < EARLY_TILES else b_banks[t - 1][:, 1, :] for t in range(PACK)]
+
+        def product_a(t):
+            first_product(a_ps[t], part(wt_w, t).bitcast(E2M1), part(wt_sc, t))
+
+        def product_b(t):
+            first_product(b_ps[t], part(w2_w, t).bitcast(E4M3), w2_sc[t])
+
+        for t in range(EARLY_TILES):
+            product_a(t)
+        for t in range(EARLY_TILES):
+            product_b(t)
+        for t in range(EARLY_TILES, PACK):
+            product_a(t)
+            product_b(t)
+
         a_sb = [tile("a%d" % t, J, F32) for t in range(PACK)]
         b_sb = [tile("b%d" % t, J, F32) for t in range(PACK)]
         lead0 = tile("lead0", 1, F32)
         nc.vector.tensor_copy(lead0[:], b_ps[0][:, 0:1])
-        leads = [lead0[:]] + [b_sb[t][:, 0:1] for t in range(1, PACK)]
+        lb = [lead0[:]] + [b_sb[t][:, 0:1] for t in range(1, PACK)]
+        la = [a_sb[t][:, 0:1] for t in range(PACK)]
         for t in range(PACK):
-            if t < 2:
+            if t < EARLY_TILES:
                 nc.scalar.activation(out=a_sb[t][:], in_=a_ps[t], func=ACT.Copy)
             else:
                 nc.vector.tensor_copy(a_sb[t][:], a_ps[t])
             nc.vector.tensor_copy(b_sb[t][:], b_ps[t])
 
-        vs_sc = tile("vs_sc", N, U8, "w2_sc")
+        vs_sc = tile("vs_sc", N, U8, reuses="w2_sc_rest")
         nc.vector.tensor_copy(vs_sc[:], vs_plane[:].indirect(idx5[:]))
 
         first = tile("first", PACK * O, F32)
         second = tile("second", PACK * O, F32)
-        diff = tile("diff", PACK * O, F32, "vs_plane")
+        diff = tile("diff", PACK * O, F32, reuses="vs_plane")
         for t in range(PACK):
-            cols = slice(t * O, (t + 1) * O)
-            nc.scalar.activation(out=first[:, cols], in_=a_sb[t][:].indirect(idx3[:]), func=ACT.Copy, scale=leads[t])
-            nc.scalar.activation(out=second[:, cols], in_=b_sb[t][:].indirect(idx4[:]), func=ACT.Copy, scale=a_sb[t][:, 0:1])
-        for cols in (slice(0, 3 * O), slice(3 * O, 4 * O)):
+            nc.scalar.activation(out=part(first, t), in_=a_sb[t][:].indirect(idx3[:]), func=ACT.Copy, scale=lb[t])
+            nc.scalar.activation(out=part(second, t), in_=b_sb[t][:].indirect(idx4[:]), func=ACT.Copy, scale=la[t])
+        last = (PACK - 1) * O
+        for cols in (slice(0, last), slice(last, PACK * O)):
             nc.vector.tensor_tensor(out=diff[:, cols], in0=first[:, cols], in1=second[:, cols], op=ALU.subtract)
 
         hid = tile("hid", O * PACK, BF16)
-        half = O // 2
         woven = hid[:].rearrange("p (o t) -> p o t", t=PACK)
-        planes = diff[:].rearrange("p (t o) -> p o t", t=PACK)
+        by_place = diff[:].rearrange("p (t o) -> p o t", t=PACK)
+        run = LINE // 4
         nc.scalar.activation(
-            out=hid[:, 0 : half * PACK].rearrange("p (c i t) -> p c t i", t=PACK, i=4),
-            in_=planes[:, 0:half, :].rearrange("p (c i) t -> p c t i", i=4),
+            out=hid[:, 0 : SCALAR_PLACES * PACK].rearrange("p (c i t) -> p c t i", t=PACK, i=run),
+            in_=by_place[:, 0:SCALAR_PLACES, :].rearrange("p (c i) t -> p c t i", i=run),
             func=ACT.Abs,
         )
+        rest = by_place[:, SCALAR_PLACES:O, :]
         nc.vector.scalar_tensor_tensor(
-            out=woven[:, half:O, :], in0=planes[:, half:O, :], scalar=-1.0, in1=planes[:, half:O, :],
-            op0=ALU.mult, op1=ALU.max,
+            out=woven[:, SCALAR_PLACES:O, :], in0=rest, scalar=-1.0, in1=rest, op0=ALU.mult, op1=ALU.max,
         )
         hid_w = tile("hid_w", O, U32)
         hid_sc = tile("hid_sc", O, U8)
         nc.vector.quantize_mx(out=hid_w[:].bitcast(E4M3), scales=hid_sc[:], in_=hid[:])
 
-        placed = []
-        for h in range(N // P):
-            cols = slice(h * P, (h + 1) * P)
-            p_ps = ps.tile([P, O], F32, name="p_ps%d" % h)
+        p_ps = []
+        for half in range(N // P):
+            acc = ps.tile([P, O], F32, name="p_ps%d" % half)
             nc.tensor.matmul_mx(
-                out=p_ps[:],
-                lhsT=vs_w[:, cols].bitcast(E2M1), lhsT_scale=vs_sc[:, cols],
+                out=acc[:],
+                lhsT=part(vs_w, half).bitcast(E2M1), lhsT_scale=part(vs_sc, half),
                 rhs=hid_w[:].bitcast(E4M3), rhs_scale=hid_sc[:],
                 start=True, stop=True,
             )
-            placed.append(p_ps)
+            p_ps.append(acc)
         p0 = tile("p0", O, F32)
-        nc.vector.tensor_copy(p0[:], placed[0][:])
+        nc.vector.tensor_copy(p0[:], p_ps[0][:])
         nc.vector.tensor_copy(pages[0][:].indirect(idx6[:]), p0[:])
         nc.sync.dma_start(out=out[0:P, :], in_=pages[0][:])
         p1 = tile("p1", O, F32)
-        nc.scalar.activation(out=p1[:], in_=placed[1][:], func=ACT.Copy)
+        nc.scalar.activation(out=p1[:], in_=p_ps[1][:], func=ACT.Copy)
         nc.scalar.activation(out=pages[1][:].indirect(idx6[:]), in_=p1[:], func=ACT.Copy)
         nc.scalar.dma_start(out=out[P : 2 * P, :], in_=pages[1][:])

from contextlib import ExitStack

import concourse.mybir as mybir

K, T, J, R, V, O, N, S, E = 512, 1024, 256, 512, 1024, 128, 256, 1024, 1024
FLOPS = 2 * (2 * K * R * J) + 2 * R * N * O

F32 = mybir.dt.float32
BF16 = mybir.dt.bfloat16
I32 = mybir.dt.int32
U32 = mybir.dt.uint32
U16 = mybir.dt.uint16
U8 = mybir.dt.uint8
E4M3 = mybir.dt.float8_e4m3fn_x4
E5M2 = mybir.dt.float8_e5m2_x4
E2M1 = mybir.dt.float4_e2m1fn_x4
ALU = mybir.AluOpType
ACT = mybir.ActivationFunctionType

P = 128
PACK = 4
QUADRANT = 32
LINE = 16
EARLY_TILES = 2
SCALAR_PLACES = 80


def tile_list_groupleads_storeleads_store_scattered_kernel(
    tc, xt_words, xt_scales, wt_words, wt_scales, w2_words, w2_scales, vs_words, vs_scales,
    offs, offs2, offs3, offs4, offs5, offs6, out,
):
    nc = tc.nc
    with ExitStack() as ctx:
        sb = ctx.enter_context(tc.tile_pool(name="sb", bufs=1))
        ps = ctx.enter_context(tc.psum_pool(name="ps", bufs=1))

        def tile(name, cols, dtype, reuses=None):
            return sb.tile([P, cols], dtype, name=name, tag=reuses or name, align_bytes=64)

        def part(whole, t):
            return whole[:, t * P : (t + 1) * P]

        def load_list(name, src):
            listed = sb.tile(list(src.shape), U16, name=name)
            nc.sync.dma_start(listed[:], src)
            return listed

        def load_words(table, words):
            nc.sync.dma_start(out=table[:].bitcast(I32), in_=words.bitcast(I32))

        def zeroed_plane(name, cols, engine):
            plane = tile(name, cols, U8)
            engine.memset(plane[:].bitcast(I32), 0)
            return plane

        def load_scales(plane, scales):
            for q in range(P // QUADRANT):
                nc.sync.dma_start(
                    out=plane[QUADRANT * q : QUADRANT * q + 4, :].bitcast(I32),
                    in_=scales[0, 4 * q : 4 * q + 4, :].bitcast(I32),
                )

        def deal(copy, dst, src, element_bytes, t0, t1):
            run = LINE // element_bytes
            copy(
                out=dst[:].rearrange("p (t c i) -> p c t i", t=t1 - t0, i=run),
                in_=src[:].rearrange("p (c i t) -> p c t i", t=PACK, i=run)[:, :, t0:t1, :],
            )

        wt_plane = zeroed_plane("wt_plane", V, nc.vector)
        w2_plane = zeroed_plane("w2_plane", R, nc.gpsimd)
        xt_plane = zeroed_plane("xt_plane", T, nc.vector)
        pages = [tile("page%d" % half, E, F32) for half in range(N // P)]
        for page in pages:
            nc.vector.memset(page[:].bitcast(I32), 0)

        xt_tab = tile("xt_tab", T, U32)
        w2_tab = tile("w2_tab", R, U32)
        wt_tab = tile("wt_tab", V, U16)
        vs_tab = tile("vs_tab", S, U16)

        load_words(wt_tab, wt_words[0])
        idx = load_list("idx", offs)
        load_scales(wt_plane, wt_scales)
        idx2 = load_list("idx2", offs2)
        load_words(xt_tab, xt_words[0].rearrange("p n t -> p (n t)"))
        load_scales(xt_plane, xt_scales)
        load_words(w2_tab, w2_words[0].rearrange("p n t -> p (n t)"))
        idx5 = load_list("idx5", offs5)
        load_words(vs_tab, vs_words[0])
        load_scales(w2_plane, w2_scales)
        vs_plane = zeroed_plane("vs_plane", S, nc.gpsimd)
        idx3 = load_list("idx3", offs3)
        idx4 = load_list("idx4", offs4)
        load_scales(vs_plane, vs_scales)
        idx6 = load_list("idx6", offs6)

        wt_listed = tile("wt_listed", R, U16)
        nc.vector.tensor_copy(wt_listed[:], wt_tab[:].indirect(idx[:]))
        wt_sc = tile("wt_sc", R, U8)
        nc.vector.tensor_copy(wt_sc[:].rearrange("p (t m) -> p m t", t=PACK), wt_plane[:].indirect(idx[:]))
        xt_w = tile("xt_w", J, U32)
        nc.vector.tensor_copy(xt_w[:], xt_tab[:].indirect(idx2[:]))
        wt_w = tile("wt_w", R, U16)
        deal(nc.vector.tensor_copy, wt_w, wt_listed, 2, 0, PACK)
        xt_sc = tile("xt_sc", J, U8)
        nc.vector.tensor_copy(xt_sc[:], xt_plane[:].indirect(idx2[:]))
        w2_w = tile("w2_w", R, U32)
        deal(nc.scalar.copy, w2_w, w2_tab, 4, 0, PACK)
        w2_sc0 = tile("w2_sc0", P, U8)
        deal(nc.vector.tensor_copy, w2_sc0, w2_plane, 1, 0, 1)
        w2_sc_rest = tile("w2_sc_rest", R - P, U8)
        deal(nc.vector.tensor_copy, w2_sc_rest, w2_plane, 1, 1, PACK)
        w2_sc = [w2_sc0[:]] + [part(w2_sc_rest, t - 1) for t in range(1, PACK)]
        vs_w = tile("vs_w", N, U16, reuses="w2_plane")
        nc.vector.tensor_copy(vs_w[:], vs_tab[:].indirect(idx5[:]))

        def first_product(acc, codes, scales):
            nc.tensor.matmul_mx(
                out=acc,
                lhsT=codes, lhsT_scale=scales,
                rhs=xt_w[:].bitcast(E5M2), rhs_scale=xt_sc[:],
                start=True, stop=True,
            )

        banks = [ps.tile([P, 2, J], F32, name="bank%d" % u) for u in range(EARLY_TILES + PACK)]
        b_banks = banks[EARLY_TILES:]
        b_ps = [bank[:, 0, :] for bank in b_banks]
        a_ps = [banks[t][:, 0, :] if t < EARLY_TILES else b_banks[t - 1][:, 1, :] for t in range(PACK)]

        def product_a(t):
            first_product(a_ps[t], part(wt_w, t).bitcast(E2M1), part(wt_sc, t))

        def product_b(t):
            first_product(b_ps[t], part(w2_w, t).bitcast(E4M3), w2_sc[t])

        for t in range(EARLY_TILES):
            product_a(t)
        for t in range(EARLY_TILES):
            product_b(t)
        for t in range(EARLY_TILES, PACK):
            product_a(t)
            product_b(t)

        a_sb = [tile("a%d" % t, J, F32) for t in range(PACK)]
        b_sb = [tile("b%d" % t, J, F32) for t in range(PACK)]
        lead0 = tile("lead0", 1, F32)
        nc.vector.tensor_copy(lead0[:], b_ps[0][:, 0:1])
        lb = [lead0[:]] + [b_sb[t][:, 0:1] for t in range(1, PACK)]
        la = [a_sb[t][:, 0:1] for t in range(PACK)]
        for t in range(PACK):
            if t < EARLY_TILES:
                nc.scalar.activation(out=a_sb[t][:], in_=a_ps[t], func=ACT.Copy)
            else:
                nc.vector.tensor_copy(a_sb[t][:], a_ps[t])
            nc.vector.tensor_copy(b_sb[t][:], b_ps[t])

        vs_sc = tile("vs_sc", N, U8, reuses="w2_sc_rest")
        nc.vector.tensor_copy(vs_sc[:], vs_plane[:].indirect(idx5[:]))

        first = tile("first", PACK * O, F32)
        second = tile("second", PACK * O, F32)
        diff = tile("diff", PACK * O, F32, reuses="vs_plane")
        for t in range(PACK):
            nc.scalar.activation(out=part(first, t), in_=a_sb[t][:].indirect(idx3[:]), func=ACT.Copy, scale=lb[t])
            nc.scalar.activation(out=part(second, t), in_=b_sb[t][:].indirect(idx4[:]), func=ACT.Copy, scale=la[t])
        last = (PACK - 1) * O
        for cols in (slice(0, last), slice(last, PACK * O)):
            nc.vector.tensor_tensor(out=diff[:, cols], in0=first[:, cols], in1=second[:, cols], op=ALU.subtract)

        hid = tile("hid", O * PACK, BF16)
        woven = hid[:].rearrange("p (o t) -> p o t", t=PACK)
        by_place = diff[:].rearrange("p (t o) -> p o t", t=PACK)
        run = LINE // 4
        nc.scalar.activation(
            out=hid[:, 0 : SCALAR_PLACES * PACK].rearrange("p (c i t) -> p c t i", t=PACK, i=run),
            in_=by_place[:, 0:SCALAR_PLACES, :].rearrange("p (c i) t -> p c t i", i=run),
            func=ACT.Abs,
        )
        rest = by_place[:, SCALAR_PLACES:O, :]
        nc.vector.scalar_tensor_tensor(
            out=woven[:, SCALAR_PLACES:O, :], in0=rest, scalar=-1.0, in1=rest, op0=ALU.mult, op1=ALU.max,
        )
        hid_w = tile("hid_w", O, U32)
        hid_sc = tile("hid_sc", O, U8)
        nc.vector.quantize_mx(out=hid_w[:].bitcast(E4M3), scales=hid_sc[:], in_=hid[:])

        p_ps = []
        for half in range(N // P):
            acc = ps.tile([P, O], F32, name="p_ps%d" % half)
            nc.tensor.matmul_mx(
                out=acc[:],
                lhsT=part(vs_w, half).bitcast(E2M1), lhsT_scale=part(vs_sc, half),
                rhs=hid_w[:].bitcast(E4M3), rhs_scale=hid_sc[:],
                start=True, stop=True,
            )
            p_ps.append(acc)
        p0 = tile("p0", O, F32)
        nc.vector.tensor_copy(p0[:], p_ps[0][:])
        nc.vector.tensor_copy(pages[0][:].indirect(idx6[:]), p0[:])
        nc.sync.dma_start(out=out[0:P, :], in_=pages[0][:])
        p1 = tile("p1", O, F32)
        nc.scalar.activation(out=p1[:], in_=p_ps[1][:], func=ACT.Copy)
        nc.scalar.activation(out=pages[1][:].indirect(idx6[:]), in_=p1[:], func=ACT.Copy)
        nc.scalar.dma_start(out=out[P : 2 * P, :], in_=pages[1][:])
